import numpy as np
import ml_dtypes


def mxq(x, axis, fmt="e4m3"):
    dtype, down = {"e4m3": (ml_dtypes.float8_e4m3fn, 7), "e5m2": (ml_dtypes.float8_e5m2, 14)}[fmt]
    v = np.moveaxis(np.asarray(x, np.float32).astype(ml_dtypes.bfloat16).astype(np.float64), axis, -1)
    blocks = v.reshape(v.shape[:-1] + (-1, 32))
    amax = np.abs(blocks).max(-1, keepdims=True)
    byte = np.maximum(np.where(amax > 0, np.frexp(amax)[1] - 1 + 127, 0) - down, 1)
    scale = np.exp2(byte - 127.0)
    codes = (blocks / scale).astype(np.float32).astype(dtype).astype(np.float64)
    return np.moveaxis((codes * scale).reshape(v.shape), -1, axis)


WIDE = False


def mx_kscale(k):
    if not WIDE:
        return np.ones(k)
    levels = np.array([10, -10, 5, -5, 0])
    if k % 512:
        return np.exp2(np.random.permutation(np.resize(levels, k // 32))).repeat(32)
    a = np.empty((k // 512, 16))
    for p in range(k // 512):
        a[p, :8] = np.random.permutation(np.resize(levels, 8))
        for g in range(8):
            far = levels[np.abs(levels - a[p, g]) >= 10]
            a[p, g + 8] = far[np.random.randint(len(far))]
    return np.exp2(a.ravel()).repeat(32)


BF16 = ml_dtypes.bfloat16


def bf(x):
    return np.asarray(x, np.float32).astype(BF16)


def f64(x):
    return np.asarray(x).astype(np.float64)


E2M1 = np.array([0.0, 0.5, 1.0, 1.5, 2.0, 3.0, 4.0, 6.0, -0.0, -0.5, -1.0, -1.5, -2.0, -3.0, -4.0, -6.0])


def pack_weight(w, fmt):
    k, n = w.shape
    w = f64(bf(w)).reshape(k // 32, 32, n)
    amax = np.abs(w).max(1)
    if fmt == "e4m3":
        byte = np.frexp(amax)[1] - 1 + 127 - 7
    else:
        mant, ex = np.frexp(amax / 6.0)
        byte = np.where(mant > 0.5, ex, ex - 1) + 127
    byte = np.clip(np.where(amax > 0, byte, 1), 1, 254)
    scaled = (w * np.exp2(127.0 - byte)[:, None, :]).reshape(k, n).astype(np.float32)
    by_word = np.ascontiguousarray(scaled.reshape(k // 512, 128, 4, n).transpose(0, 1, 3, 2))
    if fmt == "e4m3":
        words = by_word.astype(ml_dtypes.float8_e4m3fn).view(np.uint8)
    else:
        c = by_word.astype(ml_dtypes.float4_e2m1fn).view(np.uint8) & 0xF
        words = c[..., 0::2] | (c[..., 1::2] << 4)
    return np.ascontiguousarray(words), np.ascontiguousarray(byte.astype(np.uint8).reshape(k // 512, 16, n))


def unpack_weight(words, scales, fmt):
    g, p, n, _ = words.shape
    if fmt == "e4m3":
        vals = np.ascontiguousarray(words).view(ml_dtypes.float8_e4m3fn).astype(np.float64)
    else:
        nib = np.empty((g, p, n, 4), np.uint8)
        nib[..., 0::2] = words & 0xF
        nib[..., 1::2] = words >> 4
        vals = E2M1[nib]
    vals = vals * np.repeat(np.exp2(scales.astype(np.float64) - 127.0), 8, axis=1)[..., None]
    return vals.transpose(0, 1, 3, 2).reshape(g * 512, n)
def pack4(w):
    words, scales = pack_weight(w, "e2m1")
    return words.reshape(words.shape[0], 128, -1), scales


def unpack4(words, scales):
    return unpack_weight(words.reshape(words.shape[0], 128, -1, 2), scales, "e2m1")


L, H, D, R = 2048, 1024, 1024, 1536

DECAY_LOW, DECAY_HIGH = 0.5, 0.95
SKIP_SCALE = 0.5


def setup_inputs():
    s = mx_kscale(L)
    t = mx_kscale(H)
    write = np.random.standard_normal((L, H)) / np.sqrt(L) / s[:, None] * t
    value = np.random.standard_normal((L, D)) * s[:, None]
    write_words, write_scales = pack4(write)
    value_words, value_scales = pack4(value)
    return {"write_words": write_words, "write_scales": write_scales,
            "value_words": value_words, "value_scales": value_scales,
            "state": bf(np.random.standard_normal((H, D)) * t[:, None]),
            "decay": bf(np.random.uniform(DECAY_LOW, DECAY_HIGH, H)),
            "read": bf(np.random.standard_normal((R, H)) / np.sqrt(H) / t),
            "u": bf(np.random.standard_normal((R, D))),
            "skip": bf(SKIP_SCALE * np.random.standard_normal(D))}


def reference(write_words, write_scales, value_words, value_scales, state, decay, read, u, skip):
    b = unpack4(write_words, write_scales)
    x = unpack4(value_words, value_scales)
    drive = b.T @ x
    h = f64(decay)[:, None] * f64(state) + drive
    y = mxq(f64(read), 1, "e4m3") @ mxq(h, 0, "e4m3")
    return y + f64(skip) * f64(u)

@@ -1,0 +1,311 @@
+from contextlib import ExitStack
+
+import concourse.mybir as mybir
+from concourse.masks import make_identity
+
+L, H, D, R = 2048, 1024, 1024, 1536
+FLOPS = 2 * L * H * D + 2 * R * H * D
+
+F32 = mybir.dt.float32
+BF16 = mybir.dt.bfloat16
+I32 = mybir.dt.int32
+U32 = mybir.dt.uint32
+U8 = mybir.dt.uint8
+FP4X4 = mybir.dt.float4_e2m1fn_x4
+FP8X4 = mybir.dt.float8_e4m3fn_x4
+MULT = mybir.AluOpType.mult
+ADD = mybir.AluOpType.add
+
+P = 128
+PACK = 4
+SPAN = P * PACK
+PASSES = L // SPAN
+GROUPS = H // SPAN
+HALVES = D // SPAN
+PAIR = 2
+PAIRS = R // (P * PAIR)
+BANKS = 8
+ORDER = """
+B1s B1 dec U1 R0 S00 S10 X1s X1 U2 U0 R1 S01 R2 S11 R3
+U3 U5 U4 R5 R4 r00 skT r01 r02 r03 r10 r11 skC r12 W0000 W0010
+W0020 W0030 W0001 W0011 W0021 W0031 W0002 W0012 W0022 W0032 W0003 W0013 W0023 W0033 v100 r13
+u002 u001 u000 s101 d0 u003 p00 W1000 W1010 W1020 W1030 W1001 W1011 W1021 W1031 W1002
+W1012 W1022 W1032 W1003 W1013 W1023 W1033 u100 T00 T01 u101 k01 s110 s111 u102 k00
+u103 p10 s200 v211 W0110 W0111 W0112 W0113 W0120 W0121 W0122 W0123 v011 q00 W0130 W0131
+W0132 W0133 d1 W0100 W0101 W0102 W0103 Q0 d2 W1100 W1101 W1102 W1103 W1110 W1111 W1112
+W1113 T20 T21 v000 v210 q10 k20 v010 u011 u110 W1130 W1131 W1132 W1133 s001 u012
+k21 u111 u013 s201 u010 T10 T11 T30 T31 s310 u113 v311 W1120 W1121 W1122 W1123
+v301 k10 k11 Q1 Q2 k30 M000 u112 k31 e000 o000 M100 M010 M200 e100 o100
+e010 o010 M210 e200 o200 p01 M110 s500 s401 q01 p11 T50 T51 Q3 q11 e110
+o110 k50 e210 o210 T40 T41 M211 k51 M310 M011 M301 k41 e211 o211 k40 e310
+o310 s400 s300 M311 e011 o011 Q5 e301 o301 M101 e101 o101 M300 M001 e300 o300
+e001 o001 s510 M111 e111 o111 e311 o311 M201 M510 M500 M511 e510 o510 s511 Q4
+e500 o500 e201 o201 M501 M401 M411 M410 s411 e511 o511 e401 o401 M400 s501 e411
+o411 e400 o400 s410 e501 o501 e410 o410
+"""
+
+
+def tile_state_write_readout_s4_kernel(
+    tc, write_words, write_scales, value_words, value_scales, state, decay, read, u, skip, out
+):
+    nc = tc.nc
+    with ExitStack() as ctx:
+        keep = ctx.enter_context(tc.tile_pool(name="keep", bufs=1))
+        psum = ctx.enter_context(tc.psum_pool(name="psum", bufs=1))
+        ctx.enter_context(tc.manual_schedule())
+
+        def sbuf(name, shape, dtype):
+            return keep.tile(shape, dtype, name=name, align_bytes=64)
+
+        banks = [psum.tile([P, SPAN], F32, name="bank%d" % b) for b in range(BANKS)]
+        taken = []
+
+        def next_bank():
+            taken.append(len(taken) % BANKS)
+            return banks[taken[-1]]
+
+        ident = sbuf("ident", [P, P], F32)
+        decay_sb = sbuf("decay_sb", [P, GROUPS, PACK], BF16)
+        skip_rows = sbuf("skip_rows", [P, D // P], BF16)
+        skip_all = sbuf("skip_all", [P, D], BF16)
+        warm = sbuf("warm", [P, 8], F32)
+
+        b_raw = {(k, c): sbuf("b_raw%d%d" % (k, c), [P, 2, 2 * SPAN], U8) for k in range(GROUPS) for c in range(2)}
+        x_words = {(h, c): sbuf("x_words%d%d" % (h, c), [P, 2, 2 * SPAN], U8) for h in range(HALVES) for c in range(2)}
+        b_raw_scales = [sbuf("b_raw_scales%d" % k, [P, PASSES, SPAN], U8) for k in range(GROUPS)]
+        x_scales = [sbuf("x_scales%d" % h, [P, PASSES, SPAN], U8) for h in range(HALVES)]
+        b_words = {(k, g): sbuf("b_words%d%d" % (k, g), [P, PACK, 2 * P], U8) for k in range(GROUPS) for g in range(PASSES)}
+        b_scales = {(k, g): sbuf("b_scales%d%d" % (k, g), [P, PACK, P], U8) for k in range(GROUPS) for g in range(PASSES)}
+        state_sb = {(k, h): sbuf("state%d%d" % (k, h), [P, PACK, SPAN], BF16) for k in range(GROUPS) for h in range(HALVES)}
+        h_rows = {(k, h): sbuf("h_rows%d%d" % (k, h), [P, PACK, SPAN], BF16) for k in range(GROUPS) for h in range(HALVES)}
+        h_packed = {(k, h): sbuf("h_packed%d%d" % (k, h), [P, SPAN, PACK], BF16) for k in range(GROUPS) for h in range(HALVES)}
+        h_codes = {(k, h): sbuf("h_codes%d%d" % (k, h), [P, SPAN], U32) for k in range(GROUPS) for h in range(HALVES)}
+        h_scales = {(k, h): sbuf("h_scales%d%d" % (k, h), [P, SPAN], U8) for k in range(GROUPS) for h in range(HALVES)}
+        read_sb = [sbuf("read%d" % i, [P, PAIR, H], BF16) for i in range(PAIRS)]
+        packed_bufs = [sbuf("read_packed%d" % i, [P, PAIR, GROUPS, P, PACK], BF16) for i in range(3)]
+        read_packed = {}
+        split_bufs = [sbuf("read_split%d" % i, [P, PAIR, GROUPS, 2, P], F32) for i in range(3)]
+        read_split = {}
+        gate = sbuf("gate", [P, 8], U32)
+        locked = []
+        read_codes = [sbuf("read_codes%d" % i, [P, PAIR, GROUPS, P], U32) for i in range(PAIRS)]
+        read_scales = [sbuf("read_scales%d" % i, [P, PAIR, GROUPS, P], U8) for i in range(PAIRS)]
+        u_sb = [sbuf("u%d" % i, [P, PAIR, D], BF16) for i in range(PAIRS)]
+        y_sb = {(i, e, h): sbuf("y%d%d%d" % (i, e, h), [P, SPAN], F32) for i in range(PAIRS) for e in range(PAIR) for h in range(HALVES)}
+        drive = {}
+        turned = {}
+        sums = {}
+
+        def cols(i, width):
+            return slice(i * width, (i + 1) * width)
+
+        def clear(engine, plane):
+            engine.memset(plane[:].rearrange("p g n -> p (g n)").bitcast(I32), 0)
+
+        def load_words(dst, src, half, chunk):
+            rows = src.rearrange("g p n -> p g n")[:, cols(chunk, 2), cols(half, 2 * SPAN)]
+            nc.sync.dma_start(out=dst[half, chunk][:].bitcast(I32), in_=rows.bitcast(I32))
+
+        def load_scales(queue, plane, src, half, r):
+            rows = src.rearrange("g (q r) n -> r q g n", r=4)[r][:, :, cols(half, SPAN)]
+            queue.dma_start(out=plane[r:P:32, :, :].bitcast(I32), in_=rows.bitcast(I32))
+
+        def load_state(k, h):
+            rows = state[cols(k, SPAN), cols(h, SPAN)].rearrange("(p t) d -> p t d", t=PACK)
+            nc.sync.dma_start(out=state_sb[k, h][:], in_=rows)
+
+        def load_pair(dst, src, i):
+            nc.sync.dma_start(out=dst[i][:], in_=src[cols(i, P * PAIR), :].rearrange("(p e) n -> p e n", e=PAIR))
+
+        def reorder_b(k, g):
+            nc.vector.tensor_copy(
+                out=b_scales[k, g][:], in_=b_raw_scales[k][:, g, :].rearrange("p (m t) -> p t m", t=PACK)
+            )
+            nc.vector.tensor_copy(
+                out=b_words[k, g][:].rearrange("p t (m b) -> p t m b", b=2),
+                in_=b_raw[k, g // 2][:, g % 2, :].rearrange("p (m t b) -> p t m b", t=PACK, b=2),
+            )
+
+        def write_pass(k, h, t, g):
+            if g == 0:
+                drive[k, h, t] = next_bank()
+            nc.tensor.matmul_mx(
+                out=drive[k, h, t][:],
+                lhsT=b_words[k, g][:, t, :].bitcast(FP4X4),
+                lhsT_scale=b_scales[k, g][:, t, :],
+                rhs=x_words[h, g // 2][:, g % 2, :].bitcast(FP4X4),
+                rhs_scale=x_scales[h][:, g, :],
+                start=(g == 0),
+                stop=(g == PASSES - 1),
+            )
+
+        def write_by_pass(k, h):
+            for g in range(PASSES):
+                for t in range(PACK):
+                    write_pass(k, h, t, g)
+
+        def write_slot(k, h, t):
+            for g in range(PASSES):
+                write_pass(k, h, t, g)
+
+        def update(k, h, t):
+            nc.vector.scalar_tensor_tensor(
+                out=h_rows[k, h][:, t, :],
+                in0=state_sb[k, h][:, t, :],
+                scalar=decay_sb[:, k, t : t + 1],
+                in1=drive[k, h, t][:],
+                op0=MULT,
+                op1=ADD,
+            )
+
+        def pack_h(k, h):
+            nc.scalar.copy(
+                out=h_packed[k, h][:].rearrange("p (c i) t -> p c t i", i=4),
+                in_=h_rows[k, h][:].rearrange("p t (c i) -> p c t i", i=4),
+            )
+
+        def quantize_h(k, h):
+            nc.vector.quantize_mx(
+                out=h_codes[k, h][:].bitcast(FP8X4),
+                scales=h_scales[k, h][:],
+                in_=h_packed[k, h][:].rearrange("p d t -> p (d t)"),
+            )
+
+        def split_read(i):
+            read_split[i] = split_bufs[len(read_split) % 3]
+            nc.scalar.copy(
+                out=read_split[i][:].rearrange("p e k w m -> p (e k) w m"),
+                in_=read_sb[i][:].rearrange("p e n -> p (e n)").bitcast(F32).rearrange("p (c m w) -> p c w m", m=P, w=2),
+            )
+
+        def turn_read(i, e):
+            turned[i, e] = next_bank()
+            words = read_sb[i][:, e, :].bitcast(F32)
+            for k in range(GROUPS):
+                for w in range(2):
+                    src = read_split[i][:, e, k, w, :] if i in read_split else words[:, 2 * P * k + w : 2 * P * (k + 1) : 2]
+                    nc.tensor.transpose(turned[i, e][:, cols(2 * k + w, P)], src, ident[:])
+
+        def pack_read(i, e):
+            if i not in read_packed:
+                read_packed[i] = packed_bufs[len(read_packed) % 3]
+            nc.scalar.copy(
+                out=read_packed[i][:, e].bitcast(F32),
+                in_=turned[i, e][:].rearrange("p (k w r) -> p k r w", k=GROUPS, w=2),
+            )
+
+        def quantize_read(i):
+            nc.vector.quantize_mx(
+                out=read_codes[i][:].rearrange("p e k r -> p (e k r)").bitcast(FP8X4),
+                scales=read_scales[i][:].rearrange("p e k r -> p (e k r)"),
+                in_=read_packed[i][:].rearrange("p e k r t -> p (e k r t)"),
+            )
+
+        def pass_by(engine, i, e, h):
+            engine.tensor_tensor(out=y_sb[i, e, h][:], in0=u_sb[i][:, e, cols(h, SPAN)], in1=skip_all[:, cols(h, SPAN)], op=MULT)
+
+        def read_out(i, e, h):
+            sums[i, e, h] = next_bank()
+            for k in range(GROUPS):
+                nc.tensor.matmul_mx(
+                    out=sums[i, e, h][:],
+                    lhsT=read_codes[i][:, e, k, :].bitcast(FP8X4),
+                    lhsT_scale=read_scales[i][:, e, k, :],
+                    rhs=h_codes[k, h][:].bitcast(FP8X4),
+                    rhs_scale=h_scales[k, h][:],
+                    start=(k == 0),
+                    stop=(k == GROUPS - 1),
+                )
+
+        def add_sums(i, e, h):
+            nc.vector.tensor_tensor(out=y_sb[i, e, h][:], in0=sums[i, e, h][:], in1=y_sb[i, e, h][:], op=ADD)
+
+        def store(i, e, h):
+            rows = out[cols(i, P * PAIR), cols(h, SPAN)].rearrange("(p e) d -> e p d", e=PAIR)[e]
+            nc.sync.dma_start(out=rows, in_=y_sb[i, e, h][:])
+
+        clear(nc.vector, b_raw_scales[0])
+        clear(nc.vector, x_scales[0])
+        nc.gpsimd.dma_start(out=skip_rows[:], in_=skip.rearrange("(p m) -> p m", p=P))
+        load_words(b_raw, write_words, 0, 0)
+        load_words(x_words, value_words, 0, 0)
+        for r in range(4):
+            load_scales(nc.scalar, b_raw_scales[0], write_scales, 0, r)
+        for r in range(4):
+            load_scales(nc.scalar if r < 2 else nc.gpsimd, x_scales[0], value_scales, 0, r)
+        make_identity(nc, ident[:])
+        clear(nc.gpsimd, b_raw_scales[1])
+        clear(nc.gpsimd, x_scales[1])
+        nc.vector.memset(warm[:], 0.0)
+        nc.scalar.copy(out=warm[:, 4:8], in_=warm[:, 0:4])
+        load_words(b_raw, write_words, 0, 1)
+        load_words(x_words, value_words, 0, 1)
+        spread = next_bank()
+        skip_words = skip_rows[:].bitcast(F32)
+
+        for step in ORDER.split():
+            kind = step[0]
+            a = [int(c) for c in step[1:] if c in "0123456789"]
+            if step == "B1s":
+                for r in range(4):
+                    load_scales(nc.sync, b_raw_scales[1], write_scales, 1, r)
+            elif step == "X1s":
+                for r in range(4):
+                    load_scales(nc.sync, x_scales[1], value_scales, 1, r)
+            elif step == "B1":
+                for chunk in range(2):
+                    load_words(b_raw, write_words, 1, chunk)
+            elif step == "X1":
+                for chunk in range(2):
+                    load_words(x_words, value_words, 1, chunk)
+            elif step == "dec":
+                nc.sync.dma_start(out=decay_sb[:], in_=decay.rearrange("(k p t) -> p k t", p=P, t=PACK))
+            elif step == "skT":
+                for m in range(4):
+                    nc.tensor.transpose(spread[:, cols(m, P)], skip_words[:, m : m + 1].to_broadcast([P, P]), ident[:])
+            elif step == "skC":
+                nc.scalar.copy(
+                    out=skip_all[:].bitcast(F32).rearrange("p (n m) -> p n m", m=4),
+                    in_=spread[:].rearrange("p (m n) -> p n m", m=4),
+                )
+            elif kind == "S":
+                load_state(*a)
+            elif kind == "R":
+                load_pair(read_sb, read, *a)
+            elif kind == "U":
+                load_pair(u_sb, u, *a)
+            elif kind == "r":
+                reorder_b(*a)
+                locked.append(b_words[a[0], a[1]][:, 0, 0:4].bitcast(U32))
+            elif kind == "W":
+                write_pass(*a)
+            elif kind == "u":
+                update(*a)
+            elif kind == "p":
+                pack_h(*a)
+            elif kind == "q":
+                quantize_h(*a)
+                locked.append(h_codes[a[0], a[1]][:, 0:1])
+            elif kind == "d":
+                split_read(*a)
+            elif kind == "T":
+                turn_read(*a)
+            elif kind == "k":
+                pack_read(*a)
+            elif kind == "Q":
+                quantize_read(*a)
+                locked.append(read_codes[a[0]][:, 0, 0, 0:1])
+            elif kind == "v":
+                pass_by(nc.vector, *a)
+                locked.append(y_sb[a[0], a[1], a[2]][:, 0:1].bitcast(U32))
+            elif kind == "s":
+                if locked:
+                    nc.gpsimd.tensor_copy(out=gate[:, 0:1], in_=locked[-1])
+                    locked.clear()
+                pass_by(nc.gpsimd, *a)
+            elif kind == "M":
+                read_out(*a)
+            elif kind == "e":
+                add_sums(*a)
+            else:
+                store(*a)

@@ -24,24 +24,25 @@ GROUPS = H // SPAN
 HALVES = D // SPAN
 PAIR = 2
 PAIRS = R // (P * PAIR)
-BANKS = 8
+BANKS = 7
 ORDER = """
-B1s B1 dec U1 R0 S00 S10 X1s X1 U2 U0 R1 S01 R2 S11 R3
-U3 U5 U4 R5 R4 r00 skT r01 r02 r03 r10 r11 skC r12 W0000 W0010
-W0020 W0030 W0001 W0011 W0021 W0031 W0002 W0012 W0022 W0032 W0003 W0013 W0023 W0033 v100 r13
-u002 u001 u000 s101 d0 u003 p00 W1000 W1010 W1020 W1030 W1001 W1011 W1021 W1031 W1002
-W1012 W1022 W1032 W1003 W1013 W1023 W1033 u100 T00 T01 u101 k01 s110 s111 u102 k00
-u103 p10 s200 v211 W0110 W0111 W0112 W0113 W0120 W0121 W0122 W0123 v011 q00 W0130 W0131
-W0132 W0133 d1 W0100 W0101 W0102 W0103 Q0 d2 W1100 W1101 W1102 W1103 W1110 W1111 W1112
-W1113 T20 T21 v000 v210 q10 k20 v010 u011 u110 W1130 W1131 W1132 W1133 s001 u012
-k21 u111 u013 s201 u010 T10 T11 T30 T31 s310 u113 v311 W1120 W1121 W1122 W1123
-v301 k10 k11 Q1 Q2 k30 M000 u112 k31 e000 o000 M100 M010 M200 e100 o100
-e010 o010 M210 e200 o200 p01 M110 s500 s401 q01 p11 T50 T51 Q3 q11 e110
-o110 k50 e210 o210 T40 T41 M211 k51 M310 M011 M301 k41 e211 o211 k40 e310
-o310 s400 s300 M311 e011 o011 Q5 e301 o301 M101 e101 o101 M300 M001 e300 o300
-e001 o001 s510 M111 e111 o111 e311 o311 M201 M510 M500 M511 e510 o510 s511 Q4
-e500 o500 e201 o201 M501 M401 M411 M410 s411 e511 o511 e401 o401 M400 s501 e411
-o411 e400 o400 s410 e501 o501 e410 o410
+B1 B2 B3 X1 U0 X2 X3 U1 dec S00 S02 R0 U2 U3 S10 S12
+R1 R2 R3 U4 R4 R5 U5 skT skC r00 r10 c00 c01 c02 c03 c10
+c11 c12 c13 r01 r02 r03 r11 r12 r13 W0000 W0010 W0020 W0030 W0100 W0110 W0120
+W0001 W0011 W0021 W0031 W0101 W0111 W0121 W0002 W0012 W0022 W0032 W0102 W0112 W0122 W0003 W0013
+W0023 W0033 W0103 W0113 W0123 v000 v010 s001 s011 s101 s111 s201 s211 s301 s311 v100
+v110 u000 u001 u002 u003 W0130 W0131 W0132 W0133 W1000 W1001 W1002 W1003 W1010 W1011 W1012
+W1013 W1020 W1021 W1022 W1023 p00 u010 u011 u012 u013 d0 v200 v210 v300 v310 W1030
+W1031 W1032 W1033 W1100 W1101 W1102 W1103 W1110 W1111 W1112 W1113 p01 d1 u100 u101 u102
+u103 p10 T00 T01 T10 T11 u110 u111 K00 K01 k10 k11 T20 T21 k20 k21
+W1120 W1121 W1122 W1123 W1130 W1131 W1132 W1133 q00 Q0 q10 Q1 s400 s410 u112 u113
+M000 M010 M100 M110 d3 p11 e000 o000 e010 o010 T30 T31 T40 T41 e100 o100
+e110 o110 k30 k31 k40 k41 Q2 q01 q11 s401 s411 M200 M210 M201 M211 e200
+o200 e210 o210 M101 M111 e201 o201 e211 o211 M001 M011 T50 T51 e101 o101 e111
+o111 Q3 Q4 s500 s510 k50 k51 M300 M310 e001 o001 e011 o011 M301 M311 e300
+o300 e310 o310 M400 M410 e301 o301 e311 o311 Q5 s501 s511 M401 M411 e400 o400
+e410 o410 M500 M510 e401 o401 e411 o411 M501 M511 e500 o500 e510 o510 e501 o501
+e511 o511
 """
 
 
@@ -58,6 +59,7 @@ def tile_state_write_readout_s4_kernel(
             return keep.tile(shape, dtype, name=name, align_bytes=64)
 
         banks = [psum.tile([P, SPAN], F32, name="bank%d" % b) for b in range(BANKS)]
+        spread = psum.tile([P, SPAN], F32, name="spread")
         taken = []
 
         def next_bank():
@@ -68,15 +70,14 @@ def tile_state_write_readout_s4_kernel(
         decay_sb = sbuf("decay_sb", [P, GROUPS, PACK], BF16)
         skip_rows = sbuf("skip_rows", [P, D // P], BF16)
         skip_all = sbuf("skip_all", [P, D], BF16)
-        warm = sbuf("warm", [P, 8], F32)
 
-        b_raw = {(k, c): sbuf("b_raw%d%d" % (k, c), [P, 2, 2 * SPAN], U8) for k in range(GROUPS) for c in range(2)}
-        x_words = {(h, c): sbuf("x_words%d%d" % (h, c), [P, 2, 2 * SPAN], U8) for h in range(HALVES) for c in range(2)}
-        b_raw_scales = [sbuf("b_raw_scales%d" % k, [P, PASSES, SPAN], U8) for k in range(GROUPS)]
-        x_scales = [sbuf("x_scales%d" % h, [P, PASSES, SPAN], U8) for h in range(HALVES)]
+        b_raw = [sbuf("b_raw%d" % g, [P, 2 * H], U8) for g in range(PASSES)]
+        x_words = [sbuf("x_words%d" % g, [P, 2 * D], U8) for g in range(PASSES)]
+        b_raw_scales = sbuf("b_raw_scales", [P, PASSES, H], U8)
+        x_scales = sbuf("x_scales", [P, PASSES, D], U8)
         b_words = {(k, g): sbuf("b_words%d%d" % (k, g), [P, PACK, 2 * P], U8) for k in range(GROUPS) for g in range(PASSES)}
         b_scales = {(k, g): sbuf("b_scales%d%d" % (k, g), [P, PACK, P], U8) for k in range(GROUPS) for g in range(PASSES)}
-        state_sb = {(k, h): sbuf("state%d%d" % (k, h), [P, PACK, SPAN], BF16) for k in range(GROUPS) for h in range(HALVES)}
+        state_sb = {(k, c): sbuf("state%d%d" % (k, c), [P, 2, D], BF16) for k in range(GROUPS) for c in range(2)}
         h_rows = {(k, h): sbuf("h_rows%d%d" % (k, h), [P, PACK, SPAN], BF16) for k in range(GROUPS) for h in range(HALVES)}
         h_packed = {(k, h): sbuf("h_packed%d%d" % (k, h), [P, SPAN, PACK], BF16) for k in range(GROUPS) for h in range(HALVES)}
         h_codes = {(k, h): sbuf("h_codes%d%d" % (k, h), [P, SPAN], U32) for k in range(GROUPS) for h in range(HALVES)}
@@ -102,28 +103,29 @@ def tile_state_write_readout_s4_kernel(
         def clear(engine, plane):
             engine.memset(plane[:].rearrange("p g n -> p (g n)").bitcast(I32), 0)
 
-        def load_words(dst, src, half, chunk):
-            rows = src.rearrange("g p n -> p g n")[:, cols(chunk, 2), cols(half, 2 * SPAN)]
-            nc.sync.dma_start(out=dst[half, chunk][:].bitcast(I32), in_=rows.bitcast(I32))
+        def load_words(dst, src, g):
+            nc.sync.dma_start(out=dst[g][:].bitcast(I32), in_=src[g].bitcast(I32))
 
-        def load_scales(queue, plane, src, half, r):
-            rows = src.rearrange("g (q r) n -> r q g n", r=4)[r][:, :, cols(half, SPAN)]
+        def load_scales(queue, plane, src, r):
+            rows = src.rearrange("g (q r) n -> r q g n", r=4)[r]
             queue.dma_start(out=plane[r:P:32, :, :].bitcast(I32), in_=rows.bitcast(I32))
 
-        def load_state(k, h):
-            rows = state[cols(k, SPAN), cols(h, SPAN)].rearrange("(p t) d -> p t d", t=PACK)
-            nc.sync.dma_start(out=state_sb[k, h][:], in_=rows)
+        def load_state(k, t):
+            rows = state[cols(k, SPAN), :].rearrange("(p t) d -> p t d", t=PACK)[:, t : t + 2, :]
+            nc.sync.dma_start(out=state_sb[k, t // 2][:], in_=rows)
 
         def load_pair(dst, src, i):
             nc.sync.dma_start(out=dst[i][:], in_=src[cols(i, P * PAIR), :].rearrange("(p e) n -> p e n", e=PAIR))
 
+        def reorder_b_scales(k, g):
+            nc.vector.tensor_copy(
+                out=b_scales[k, g][:], in_=b_raw_scales[:, g, cols(k, SPAN)].rearrange("p (m t) -> p t m", t=PACK)
+            )
+
         def reorder_b(k, g):
             nc.vector.tensor_copy(
-                out=b_scales[k, g][:], in_=b_raw_scales[k][:, g, :].rearrange("p (m t) -> p t m", t=PACK)
-            )
-            nc.vector.tensor_copy(
                 out=b_words[k, g][:].rearrange("p t (m b) -> p t m b", b=2),
-                in_=b_raw[k, g // 2][:, g % 2, :].rearrange("p (m t b) -> p t m b", t=PACK, b=2),
+                in_=b_raw[g][:, cols(k, 2 * SPAN)].rearrange("p (m t b) -> p t m b", t=PACK, b=2),
             )
 
         def write_pass(k, h, t, g):
@@ -133,8 +135,8 @@ def tile_state_write_readout_s4_kernel(
                 out=drive[k, h, t][:],
                 lhsT=b_words[k, g][:, t, :].bitcast(FP4X4),
                 lhsT_scale=b_scales[k, g][:, t, :],
-                rhs=x_words[h, g // 2][:, g % 2, :].bitcast(FP4X4),
-                rhs_scale=x_scales[h][:, g, :],
+                rhs=x_words[g][:, cols(h, 2 * SPAN)].bitcast(FP4X4),
+                rhs_scale=x_scales[:, g, cols(h, SPAN)],
                 start=(g == 0),
                 stop=(g == PASSES - 1),
             )
@@ -151,15 +153,15 @@ def tile_state_write_readout_s4_kernel(
         def update(k, h, t):
             nc.vector.scalar_tensor_tensor(
                 out=h_rows[k, h][:, t, :],
-                in0=state_sb[k, h][:, t, :],
+                in0=state_sb[k, t // 2][:, t % 2, cols(h, SPAN)],
                 scalar=decay_sb[:, k, t : t + 1],
                 in1=drive[k, h, t][:],
                 op0=MULT,
                 op1=ADD,
             )
 
-        def pack_h(k, h):
-            nc.scalar.copy(
+        def pack_h(copy, k, h):
+            copy(
                 out=h_packed[k, h][:].rearrange("p (c i) t -> p c t i", i=4),
                 in_=h_rows[k, h][:].rearrange("p t (c i) -> p c t i", i=4),
             )
@@ -186,10 +188,10 @@ def tile_state_write_readout_s4_kernel(
                     src = read_split[i][:, e, k, w, :] if i in read_split else words[:, 2 * P * k + w : 2 * P * (k + 1) : 2]
                     nc.tensor.transpose(turned[i, e][:, cols(2 * k + w, P)], src, ident[:])
 
-        def pack_read(i, e):
+        def pack_read(copy, i, e):
             if i not in read_packed:
                 read_packed[i] = packed_bufs[len(read_packed) % 3]
-            nc.scalar.copy(
+            copy(
                 out=read_packed[i][:, e].bitcast(F32),
                 in_=turned[i, e][:].rearrange("p (k w r) -> p k r w", k=GROUPS, w=2),
             )
@@ -201,8 +203,17 @@ def tile_state_write_readout_s4_kernel(
                 in_=read_packed[i][:].rearrange("p e k r t -> p (e k r t)"),
             )
 
-        def pass_by(engine, i, e, h):
-            engine.tensor_tensor(out=y_sb[i, e, h][:], in0=u_sb[i][:, e, cols(h, SPAN)], in1=skip_all[:, cols(h, SPAN)], op=MULT)
+        def pass_by_gpsimd(i, e, h):
+            nc.gpsimd.tensor_tensor(out=y_sb[i, e, h][:], in0=u_sb[i][:, e, cols(h, SPAN)], in1=skip_all[:, cols(h, SPAN)], op=MULT)
+
+        def pass_by_vector(i, e, h):
+            skip_psum = spread[:].bitcast(BF16).rearrange("p (m n s) -> p n m s", m=4, s=2)[:, cols(h, P // HALVES)]
+            nc.vector.tensor_tensor(
+                out=y_sb[i, e, h][:].rearrange("p (n m s) -> p n m s", m=4, s=2),
+                in0=u_sb[i][:, e, cols(h, SPAN)].rearrange("p (n m s) -> p n m s", m=4, s=2),
+                in1=skip_psum,
+                op=MULT,
+            )
 
         def read_out(i, e, h):
             sums[i, e, h] = next_bank()
@@ -224,42 +235,28 @@ def tile_state_write_readout_s4_kernel(
             rows = out[cols(i, P * PAIR), cols(h, SPAN)].rearrange("(p e) d -> e p d", e=PAIR)[e]
             nc.sync.dma_start(out=rows, in_=y_sb[i, e, h][:])
 
-        clear(nc.vector, b_raw_scales[0])
-        clear(nc.vector, x_scales[0])
-        nc.gpsimd.dma_start(out=skip_rows[:], in_=skip.rearrange("(p m) -> p m", p=P))
-        load_words(b_raw, write_words, 0, 0)
-        load_words(x_words, value_words, 0, 0)
+        clear(nc.vector, b_raw_scales)
+        clear(nc.vector, x_scales)
+        nc.vector.memset(ident[:], 0.0)
+        make_identity(nc, ident[:], nomemset=True)
+        nc.sync.dma_start(out=skip_rows[:], in_=skip.rearrange("(p m) -> p m", p=P))
+        load_words(b_raw, write_words, 0)
+        load_words(x_words, value_words, 0)
         for r in range(4):
-            load_scales(nc.scalar, b_raw_scales[0], write_scales, 0, r)
+            load_scales(nc.sync, b_raw_scales, write_scales, r)
         for r in range(4):
-            load_scales(nc.scalar if r < 2 else nc.gpsimd, x_scales[0], value_scales, 0, r)
-        make_identity(nc, ident[:])
-        clear(nc.gpsimd, b_raw_scales[1])
-        clear(nc.gpsimd, x_scales[1])
-        nc.vector.memset(warm[:], 0.0)
-        nc.scalar.copy(out=warm[:, 4:8], in_=warm[:, 0:4])
-        load_words(b_raw, write_words, 0, 1)
-        load_words(x_words, value_words, 0, 1)
-        spread = next_bank()
+            load_scales(nc.sync, x_scales, value_scales, r)
         skip_words = skip_rows[:].bitcast(F32)
 
         for step in ORDER.split():
             kind = step[0]
             a = [int(c) for c in step[1:] if c in "0123456789"]
-            if step == "B1s":
-                for r in range(4):
-                    load_scales(nc.sync, b_raw_scales[1], write_scales, 1, r)
-            elif step == "X1s":
-                for r in range(4):
-                    load_scales(nc.sync, x_scales[1], value_scales, 1, r)
-            elif step == "B1":
-                for chunk in range(2):
-                    load_words(b_raw, write_words, 1, chunk)
-            elif step == "X1":
-                for chunk in range(2):
-                    load_words(x_words, value_words, 1, chunk)
+            if kind == "B":
+                load_words(b_raw, write_words, *a)
             elif step == "dec":
                 nc.sync.dma_start(out=decay_sb[:], in_=decay.rearrange("(k p t) -> p k t", p=P, t=PACK))
+            elif kind == "X":
+                load_words(x_words, value_words, *a)
             elif step == "skT":
                 for m in range(4):
                     nc.tensor.transpose(spread[:, cols(m, P)], skip_words[:, m : m + 1].to_broadcast([P, P]), ident[:])
@@ -277,12 +274,17 @@ def tile_state_write_readout_s4_kernel(
             elif kind == "r":
                 reorder_b(*a)
                 locked.append(b_words[a[0], a[1]][:, 0, 0:4].bitcast(U32))
+            elif kind == "c":
+                reorder_b_scales(*a)
             elif kind == "W":
                 write_pass(*a)
             elif kind == "u":
                 update(*a)
             elif kind == "p":
-                pack_h(*a)
+                pack_h(nc.scalar.copy, *a)
+            elif kind == "P":
+                pack_h(nc.vector.tensor_copy, *a)
+                locked.append(h_packed[a[0], a[1]][:, 0, 0:2].bitcast(U32))
             elif kind == "q":
                 quantize_h(*a)
                 locked.append(h_codes[a[0], a[1]][:, 0:1])
@@ -291,18 +293,19 @@ def tile_state_write_readout_s4_kernel(
             elif kind == "T":
                 turn_read(*a)
             elif kind == "k":
-                pack_read(*a)
+                pack_read(nc.scalar.copy, *a)
+            elif kind == "K":
+                pack_read(nc.vector.tensor_copy, *a)
             elif kind == "Q":
                 quantize_read(*a)
                 locked.append(read_codes[a[0]][:, 0, 0, 0:1])
             elif kind == "v":
-                pass_by(nc.vector, *a)
-                locked.append(y_sb[a[0], a[1], a[2]][:, 0:1].bitcast(U32))
+                pass_by_vector(*a)
             elif kind == "s":
                 if locked:
                     nc.gpsimd.tensor_copy(out=gate[:, 0:1], in_=locked[-1])
                     locked.clear()
-                pass_by(nc.gpsimd, *a)
+                pass_by_gpsimd(*a)
             elif kind == "M":
                 read_out(*a)
             elif kind == "e":

from contextlib import ExitStack

import concourse.mybir as mybir
from concourse.masks import make_identity

L, H, D, R = 2048, 1024, 1024, 1536
FLOPS = 2 * L * H * D + 2 * R * H * D

F32 = mybir.dt.float32
BF16 = mybir.dt.bfloat16
I32 = mybir.dt.int32
U32 = mybir.dt.uint32
U8 = mybir.dt.uint8
FP4X4 = mybir.dt.float4_e2m1fn_x4
FP8X4 = mybir.dt.float8_e4m3fn_x4
MULT = mybir.AluOpType.mult
ADD = mybir.AluOpType.add

P = 128
PACK = 4
SPAN = P * PACK
PASSES = L // SPAN
GROUPS = H // SPAN
HALVES = D // SPAN
PAIR = 2
PAIRS = R // (P * PAIR)
BANKS = 7
ORDER = """
B1 B2 B3 X1 U0 X2 X3 U1 dec S00 S02 R0 U2 U3 S10 S12
R1 R2 R3 U4 R4 R5 U5 skT skC r00 r10 c00 c01 c02 c03 c10
c11 c12 c13 r01 r02 r03 r11 r12 r13 W0000 W0010 W0020 W0030 W0100 W0110 W0120
W0001 W0011 W0021 W0031 W0101 W0111 W0121 W0002 W0012 W0022 W0032 W0102 W0112 W0122 W0003 W0013
W0023 W0033 W0103 W0113 W0123 v000 v010 s001 s011 s101 s111 s201 s211 s301 s311 v100
v110 u000 u001 u002 u003 W0130 W0131 W0132 W0133 W1000 W1001 W1002 W1003 W1010 W1011 W1012
W1013 W1020 W1021 W1022 W1023 p00 u010 u011 u012 u013 d0 v200 v210 v300 v310 W1030
W1031 W1032 W1033 W1100 W1101 W1102 W1103 W1110 W1111 W1112 W1113 p01 d1 u100 u101 u102
u103 p10 T00 T01 T10 T11 u110 u111 K00 K01 k10 k11 T20 T21 k20 k21
W1120 W1121 W1122 W1123 W1130 W1131 W1132 W1133 q00 Q0 q10 Q1 s400 s410 u112 u113
M000 M010 M100 M110 d3 p11 e000 o000 e010 o010 T30 T31 T40 T41 e100 o100
e110 o110 k30 k31 k40 k41 Q2 q01 q11 s401 s411 M200 M210 M201 M211 e200
o200 e210 o210 M101 M111 e201 o201 e211 o211 M001 M011 T50 T51 e101 o101 e111
o111 Q3 Q4 s500 s510 k50 k51 M300 M310 e001 o001 e011 o011 M301 M311 e300
o300 e310 o310 M400 M410 e301 o301 e311 o311 Q5 s501 s511 M401 M411 e400 o400
e410 o410 M500 M510 e401 o401 e411 o411 M501 M511 e500 o500 e510 o510 e501 o501
e511 o511
"""


def tile_state_write_readout_s4_kernel(
    tc, write_words, write_scales, value_words, value_scales, state, decay, read, u, skip, out
):
    nc = tc.nc
    with ExitStack() as ctx:
        keep = ctx.enter_context(tc.tile_pool(name="keep", bufs=1))
        psum = ctx.enter_context(tc.psum_pool(name="psum", bufs=1))
        ctx.enter_context(tc.manual_schedule())

        def sbuf(name, shape, dtype):
            return keep.tile(shape, dtype, name=name, align_bytes=64)

        banks = [psum.tile([P, SPAN], F32, name="bank%d" % b) for b in range(BANKS)]
        spread = psum.tile([P, SPAN], F32, name="spread")
        taken = []

        def next_bank():
            taken.append(len(taken) % BANKS)
            return banks[taken[-1]]

        ident = sbuf("ident", [P, P], F32)
        decay_sb = sbuf("decay_sb", [P, GROUPS, PACK], BF16)
        skip_rows = sbuf("skip_rows", [P, D // P], BF16)
        skip_all = sbuf("skip_all", [P, D], BF16)

        b_raw = [sbuf("b_raw%d" % g, [P, 2 * H], U8) for g in range(PASSES)]
        x_words = [sbuf("x_words%d" % g, [P, 2 * D], U8) for g in range(PASSES)]
        b_raw_scales = sbuf("b_raw_scales", [P, PASSES, H], U8)
        x_scales = sbuf("x_scales", [P, PASSES, D], U8)
        b_words = {(k, g): sbuf("b_words%d%d" % (k, g), [P, PACK, 2 * P], U8) for k in range(GROUPS) for g in range(PASSES)}
        b_scales = {(k, g): sbuf("b_scales%d%d" % (k, g), [P, PACK, P], U8) for k in range(GROUPS) for g in range(PASSES)}
        state_sb = {(k, c): sbuf("state%d%d" % (k, c), [P, 2, D], BF16) for k in range(GROUPS) for c in range(2)}
        h_rows = {(k, h): sbuf("h_rows%d%d" % (k, h), [P, PACK, SPAN], BF16) for k in range(GROUPS) for h in range(HALVES)}
        h_packed = {(k, h): sbuf("h_packed%d%d" % (k, h), [P, SPAN, PACK], BF16) for k in range(GROUPS) for h in range(HALVES)}
        h_codes = {(k, h): sbuf("h_codes%d%d" % (k, h), [P, SPAN], U32) for k in range(GROUPS) for h in range(HALVES)}
        h_scales = {(k, h): sbuf("h_scales%d%d" % (k, h), [P, SPAN], U8) for k in range(GROUPS) for h in range(HALVES)}
        read_sb = [sbuf("read%d" % i, [P, PAIR, H], BF16) for i in range(PAIRS)]
        packed_bufs = [sbuf("read_packed%d" % i, [P, PAIR, GROUPS, P, PACK], BF16) for i in range(3)]
        read_packed = {}
        split_bufs = [sbuf("read_split%d" % i, [P, PAIR, GROUPS, 2, P], F32) for i in range(3)]
        read_split = {}
        gate = sbuf("gate", [P, 8], U32)
        locked = []
        read_codes = [sbuf("read_codes%d" % i, [P, PAIR, GROUPS, P], U32) for i in range(PAIRS)]
        read_scales = [sbuf("read_scales%d" % i, [P, PAIR, GROUPS, P], U8) for i in range(PAIRS)]
        u_sb = [sbuf("u%d" % i, [P, PAIR, D], BF16) for i in range(PAIRS)]
        y_sb = {(i, e, h): sbuf("y%d%d%d" % (i, e, h), [P, SPAN], F32) for i in range(PAIRS) for e in range(PAIR) for h in range(HALVES)}
        drive = {}
        turned = {}
        sums = {}

        def cols(i, width):
            return slice(i * width, (i + 1) * width)

        def clear(engine, plane):
            engine.memset(plane[:].rearrange("p g n -> p (g n)").bitcast(I32), 0)

        def load_words(dst, src, g):
            nc.sync.dma_start(out=dst[g][:].bitcast(I32), in_=src[g].bitcast(I32))

        def load_scales(queue, plane, src, r):
            rows = src.rearrange("g (q r) n -> r q g n", r=4)[r]
            queue.dma_start(out=plane[r:P:32, :, :].bitcast(I32), in_=rows.bitcast(I32))

        def load_state(k, t):
            rows = state[cols(k, SPAN), :].rearrange("(p t) d -> p t d", t=PACK)[:, t : t + 2, :]
            nc.sync.dma_start(out=state_sb[k, t // 2][:], in_=rows)

        def load_pair(dst, src, i):
            nc.sync.dma_start(out=dst[i][:], in_=src[cols(i, P * PAIR), :].rearrange("(p e) n -> p e n", e=PAIR))

        def reorder_b_scales(k, g):
            nc.vector.tensor_copy(
                out=b_scales[k, g][:], in_=b_raw_scales[:, g, cols(k, SPAN)].rearrange("p (m t) -> p t m", t=PACK)
            )

        def reorder_b(k, g):
            nc.vector.tensor_copy(
                out=b_words[k, g][:].rearrange("p t (m b) -> p t m b", b=2),
                in_=b_raw[g][:, cols(k, 2 * SPAN)].rearrange("p (m t b) -> p t m b", t=PACK, b=2),
            )

        def write_pass(k, h, t, g):
            if g == 0:
                drive[k, h, t] = next_bank()
            nc.tensor.matmul_mx(
                out=drive[k, h, t][:],
                lhsT=b_words[k, g][:, t, :].bitcast(FP4X4),
                lhsT_scale=b_scales[k, g][:, t, :],
                rhs=x_words[g][:, cols(h, 2 * SPAN)].bitcast(FP4X4),
                rhs_scale=x_scales[:, g, cols(h, SPAN)],
                start=(g == 0),
                stop=(g == PASSES - 1),
            )

        def write_by_pass(k, h):
            for g in range(PASSES):
                for t in range(PACK):
                    write_pass(k, h, t, g)

        def write_slot(k, h, t):
            for g in range(PASSES):
                write_pass(k, h, t, g)

        def update(k, h, t):
            nc.vector.scalar_tensor_tensor(
                out=h_rows[k, h][:, t, :],
                in0=state_sb[k, t // 2][:, t % 2, cols(h, SPAN)],
                scalar=decay_sb[:, k, t : t + 1],
                in1=drive[k, h, t][:],
                op0=MULT,
                op1=ADD,
            )

        def pack_h(copy, k, h):
            copy(
                out=h_packed[k, h][:].rearrange("p (c i) t -> p c t i", i=4),
                in_=h_rows[k, h][:].rearrange("p t (c i) -> p c t i", i=4),
            )

        def quantize_h(k, h):
            nc.vector.quantize_mx(
                out=h_codes[k, h][:].bitcast(FP8X4),
                scales=h_scales[k, h][:],
                in_=h_packed[k, h][:].rearrange("p d t -> p (d t)"),
            )

        def split_read(i):
            read_split[i] = split_bufs[len(read_split) % 3]
            nc.scalar.copy(
                out=read_split[i][:].rearrange("p e k w m -> p (e k) w m"),
                in_=read_sb[i][:].rearrange("p e n -> p (e n)").bitcast(F32).rearrange("p (c m w) -> p c w m", m=P, w=2),
            )

        def turn_read(i, e):
            turned[i, e] = next_bank()
            words = read_sb[i][:, e, :].bitcast(F32)
            for k in range(GROUPS):
                for w in range(2):
                    src = read_split[i][:, e, k, w, :] if i in read_split else words[:, 2 * P * k + w : 2 * P * (k + 1) : 2]
                    nc.tensor.transpose(turned[i, e][:, cols(2 * k + w, P)], src, ident[:])

        def pack_read(copy, i, e):
            if i not in read_packed:
                read_packed[i] = packed_bufs[len(read_packed) % 3]
            copy(
                out=read_packed[i][:, e].bitcast(F32),
                in_=turned[i, e][:].rearrange("p (k w r) -> p k r w", k=GROUPS, w=2),
            )

        def quantize_read(i):
            nc.vector.quantize_mx(
                out=read_codes[i][:].rearrange("p e k r -> p (e k r)").bitcast(FP8X4),
                scales=read_scales[i][:].rearrange("p e k r -> p (e k r)"),
                in_=read_packed[i][:].rearrange("p e k r t -> p (e k r t)"),
            )

        def pass_by_gpsimd(i, e, h):
            nc.gpsimd.tensor_tensor(out=y_sb[i, e, h][:], in0=u_sb[i][:, e, cols(h, SPAN)], in1=skip_all[:, cols(h, SPAN)], op=MULT)

        def pass_by_vector(i, e, h):
            skip_psum = spread[:].bitcast(BF16).rearrange("p (m n s) -> p n m s", m=4, s=2)[:, cols(h, P // HALVES)]
            nc.vector.tensor_tensor(
                out=y_sb[i, e, h][:].rearrange("p (n m s) -> p n m s", m=4, s=2),
                in0=u_sb[i][:, e, cols(h, SPAN)].rearrange("p (n m s) -> p n m s", m=4, s=2),
                in1=skip_psum,
                op=MULT,
            )

        def read_out(i, e, h):
            sums[i, e, h] = next_bank()
            for k in range(GROUPS):
                nc.tensor.matmul_mx(
                    out=sums[i, e, h][:],
                    lhsT=read_codes[i][:, e, k, :].bitcast(FP8X4),
                    lhsT_scale=read_scales[i][:, e, k, :],
                    rhs=h_codes[k, h][:].bitcast(FP8X4),
                    rhs_scale=h_scales[k, h][:],
                    start=(k == 0),
                    stop=(k == GROUPS - 1),
                )

        def add_sums(i, e, h):
            nc.vector.tensor_tensor(out=y_sb[i, e, h][:], in0=sums[i, e, h][:], in1=y_sb[i, e, h][:], op=ADD)

        def store(i, e, h):
            rows = out[cols(i, P * PAIR), cols(h, SPAN)].rearrange("(p e) d -> e p d", e=PAIR)[e]
            nc.sync.dma_start(out=rows, in_=y_sb[i, e, h][:])

        clear(nc.vector, b_raw_scales)
        clear(nc.vector, x_scales)
        nc.vector.memset(ident[:], 0.0)
        make_identity(nc, ident[:], nomemset=True)
        nc.sync.dma_start(out=skip_rows[:], in_=skip.rearrange("(p m) -> p m", p=P))
        load_words(b_raw, write_words, 0)
        load_words(x_words, value_words, 0)
        for r in range(4):
            load_scales(nc.sync, b_raw_scales, write_scales, r)
        for r in range(4):
            load_scales(nc.sync, x_scales, value_scales, r)
        skip_words = skip_rows[:].bitcast(F32)

        for step in ORDER.split():
            kind = step[0]
            a = [int(c) for c in step[1:] if c in "0123456789"]
            if kind == "B":
                load_words(b_raw, write_words, *a)
            elif step == "dec":
                nc.sync.dma_start(out=decay_sb[:], in_=decay.rearrange("(k p t) -> p k t", p=P, t=PACK))
            elif kind == "X":
                load_words(x_words, value_words, *a)
            elif step == "skT":
                for m in range(4):
                    nc.tensor.transpose(spread[:, cols(m, P)], skip_words[:, m : m + 1].to_broadcast([P, P]), ident[:])
            elif step == "skC":
                nc.scalar.copy(
                    out=skip_all[:].bitcast(F32).rearrange("p (n m) -> p n m", m=4),
                    in_=spread[:].rearrange("p (m n) -> p n m", m=4),
                )
            elif kind == "S":
                load_state(*a)
            elif kind == "R":
                load_pair(read_sb, read, *a)
            elif kind == "U":
                load_pair(u_sb, u, *a)
            elif kind == "r":
                reorder_b(*a)
                locked.append(b_words[a[0], a[1]][:, 0, 0:4].bitcast(U32))
            elif kind == "c":
                reorder_b_scales(*a)
            elif kind == "W":
                write_pass(*a)
            elif kind == "u":
                update(*a)
            elif kind == "p":
                pack_h(nc.scalar.copy, *a)
            elif kind == "P":
                pack_h(nc.vector.tensor_copy, *a)
                locked.append(h_packed[a[0], a[1]][:, 0, 0:2].bitcast(U32))
            elif kind == "q":
                quantize_h(*a)
                locked.append(h_codes[a[0], a[1]][:, 0:1])
            elif kind == "d":
                split_read(*a)
            elif kind == "T":
                turn_read(*a)
            elif kind == "k":
                pack_read(nc.scalar.copy, *a)
            elif kind == "K":
                pack_read(nc.vector.tensor_copy, *a)
            elif kind == "Q":
                quantize_read(*a)
                locked.append(read_codes[a[0]][:, 0, 0, 0:1])
            elif kind == "v":
                pass_by_vector(*a)
            elif kind == "s":
                if locked:
                    nc.gpsimd.tensor_copy(out=gate[:, 0:1], in_=locked[-1])
                    locked.clear()
                pass_by_gpsimd(*a)
            elif kind == "M":
                read_out(*a)
            elif kind == "e":
                add_sums(*a)
            else:
                store(*a)
